import numpy as np
import ml_dtypes


def mxq(x, axis, fmt="e4m3"):
    dtype, down = {"e4m3": (ml_dtypes.float8_e4m3fn, 7), "e5m2": (ml_dtypes.float8_e5m2, 14)}[fmt]
    v = np.moveaxis(np.asarray(x, np.float32).astype(ml_dtypes.bfloat16).astype(np.float64), axis, -1)
    blocks = v.reshape(v.shape[:-1] + (-1, 32))
    amax = np.abs(blocks).max(-1, keepdims=True)
    byte = np.maximum(np.where(amax > 0, np.frexp(amax)[1] - 1 + 127, 0) - down, 1)
    scale = np.exp2(byte - 127.0)
    codes = (blocks / scale).astype(np.float32).astype(dtype).astype(np.float64)
    return np.moveaxis((codes * scale).reshape(v.shape), -1, axis)


WIDE = False


def mx_kscale(k):
    if not WIDE:
        return np.ones(k)
    levels = np.array([10, -10, 5, -5, 0])
    if k % 512:
        return np.exp2(np.random.permutation(np.resize(levels, k // 32))).repeat(32)
    a = np.empty((k // 512, 16))
    for p in range(k // 512):
        a[p, :8] = np.random.permutation(np.resize(levels, 8))
        for g in range(8):
            far = levels[np.abs(levels - a[p, g]) >= 10]
            a[p, g + 8] = far[np.random.randint(len(far))]
    return np.exp2(a.ravel()).repeat(32)


def f64(x):
    return np.asarray(x).astype(np.float64)


def striped(idx):
    return np.tile(np.asarray(idx).reshape(-1, 16).T, (8, 1)).astype(np.uint16)


def unstriped(offs):
    return offs[:16].T.reshape(-1).astype(np.int64)


def striped8(idx):
    return np.asarray(idx).reshape(8, -1, 16).transpose(0, 2, 1).reshape(128, -1).astype(np.uint16)


def unstriped8(offs):
    return offs.reshape(8, 16, -1).transpose(0, 2, 1).reshape(8, -1).astype(np.int64)


def pick8(x, idx, run):
    r = np.arange(len(x))
    return x[r[:, None], idx[r % (8 * run) // run]]


E2M1 = np.array([0.0, 0.5, 1.0, 1.5, 2.0, 3.0, 4.0, 6.0, -0.0, -0.5, -1.0, -1.5, -2.0, -3.0, -4.0, -6.0])


def pack_weight(w, fmt):
    k, n = w.shape
    w = f64(np.asarray(w, np.float32).astype(ml_dtypes.bfloat16)).reshape(k // 32, 32, n)
    amax = np.abs(w).max(1)
    if fmt == "e4m3":
        byte = np.frexp(amax)[1] - 1 + 127 - 7
    else:
        mant, ex = np.frexp(amax / 6.0)
        byte = np.where(mant > 0.5, ex, ex - 1) + 127
    byte = np.clip(np.where(amax > 0, byte, 1), 1, 254)
    scaled = (w * np.exp2(127.0 - byte)[:, None, :]).reshape(k, n).astype(np.float32)
    by_word = np.ascontiguousarray(scaled.reshape(k // 512, 128, 4, n).transpose(0, 1, 3, 2))
    if fmt == "e4m3":
        words = by_word.astype(ml_dtypes.float8_e4m3fn).view(np.uint8)
    else:
        c = by_word.astype(ml_dtypes.float4_e2m1fn).view(np.uint8) & 0xF
        words = (c[..., 0::2] | (c[..., 1::2] << 4)).reshape(k // 512, 128, 2 * n)
    return np.ascontiguousarray(words), np.ascontiguousarray(byte.astype(np.uint8).reshape(k // 512, 16, n))


def unpack_weight(words, scales, fmt):
    g, _, n = scales.shape
    words = np.ascontiguousarray(words).reshape(g, 128, n, -1)
    if fmt == "e4m3":
        vals = words.view(ml_dtypes.float8_e4m3fn).astype(np.float64)
    else:
        nib = np.empty((g, 128, n, 4), np.uint8)
        nib[..., 0::2] = words & 0xF
        nib[..., 1::2] = words >> 4
        vals = E2M1[nib]
    vals = vals * np.repeat(np.exp2(scales.astype(np.float64) - 127.0), 8, axis=1)[..., None]
    return vals.transpose(0, 1, 3, 2).reshape(g * 512, n)


K, J, R, T, Z, M, O, N, U, E = 512, 512, 512, 2048, 512, 1024, 256, 256, 128, 512


def setup_inputs():
    n = np.random.standard_normal
    idx = np.stack([np.random.permutation(T)[:J] for _ in range(8)])
    idx2 = np.random.permutation(M)[:J]
    idx3 = np.random.permutation(J)[:O]
    idx4 = np.stack([np.random.permutation(J)[:O] for _ in range(8)])
    idx5 = np.random.permutation(E)[:O]
    idx6 = np.stack([np.random.permutation(E)[:U] for _ in range(8)])
    idx7 = np.stack([np.random.permutation(O)[:U] for _ in range(8)])
    fk = mx_kscale(K)
    fr = mx_kscale(R)
    fz = mx_kscale(Z)
    wp = pack_weight(n((K, R)) * 1 / np.sqrt(K) / fk[:, None] * fr, "e2m1")
    xop = pack_weight(n((Z, M)) / fz[:, None], "e2m1")
    w2p = pack_weight(n((Z, R)) * 1 / np.sqrt(Z) * fz[:, None] * fr, "e4m3")
    wbp = pack_weight(n((R, N)) * 1 / np.sqrt(R) / fr[:, None], "e4m3")
    wop = pack_weight(n((R, N)) * 1 / np.sqrt(R) / fr[:, None], "e2m1")
    return {
        "ta": (np.random.randint(-7, 8, (K, T)).astype(np.float64)).astype(np.float32),
        "ga": ((np.random.randint(8, 25, (K, 1)) / 64.0) * fk[:, None]).astype(np.float32),
        "w_words": wp[0],
        "w_scales": wp[1],
        "xo_words": xop[0],
        "xo_scales": xop[1],
        "w2_words": w2p[0],
        "w2_scales": w2p[1],
        "sa": (np.random.uniform(0.5, 1.6, (R, 1))).astype(np.float32),
        "sb": (np.random.uniform(0.5, 1.6, (R, 1))).astype(np.float32),
        "wb_words": wbp[0],
        "wb_scales": wbp[1],
        "wo_words": wop[0],
        "wo_scales": wop[1],
        "so": (np.random.uniform(0.5, 1.6, (N, 1))).astype(np.float32),
        "sp": (np.random.uniform(0.5, 1.6, (N, 1))).astype(np.float32),
        "offs": striped8(idx),
        "offs2": striped(idx2),
        "offs3": striped(idx3),
        "offs4": striped8(idx4),
        "offs5": striped(idx5),
        "offs6": striped8(idx6),
        "offs7": striped8(idx7),
    }


def reference(ta, ga, w_words, w_scales, xo_words, xo_scales, w2_words, w2_scales, sa, sb, wb_words, wb_scales, wo_words, wo_scales, so, sp, offs, offs2, offs3, offs4, offs5, offs6, offs7):
    idx = unstriped8(offs)
    idx2 = unstriped(offs2)
    idx3 = unstriped(offs3)
    idx4 = unstriped8(offs4)
    idx5 = unstriped(offs5)
    idx6 = unstriped8(offs6)
    idx7 = unstriped8(offs7)
    wu = unpack_weight(w_words, w_scales, "e2m1")
    xou = unpack_weight(xo_words, xo_scales, "e2m1")
    w2u = unpack_weight(w2_words, w2_scales, "e4m3")
    wbu = unpack_weight(wb_words, wb_scales, "e4m3")
    wou = unpack_weight(wo_words, wo_scales, "e2m1")
    xc = pick8(f64(ta), idx, 64) * f64(ga)
    xcq = mxq(xc, 0, "e4m3")
    xoidx2g = xou[:, idx2]
    a = wu.T @ xcq + w2u.T @ xoidx2g
    hid = np.abs(a[:, idx3] * f64(sa) - pick8(a, idx4, 64) * f64(sb))
    hidq = mxq(hid, 0, "e4m3")
    p = wbu.T @ hidq
    q = wou.T @ hidq
    m0 = np.zeros((N, E))
    m0[:, idx5] = p
    y = np.maximum(pick8(m0, idx6, 16) * f64(so), pick8(q, idx7, 16) * f64(sp))
    return y

@@ -1,0 +1,264 @@
+from contextlib import ExitStack
+
+import concourse.mybir as mybir
+
+K, J, R, T, Z, M, O, N, U, E = 512, 512, 512, 2048, 512, 1024, 256, 256, 128, 512
+FLOPS = 2 * (K * R * J + Z * R * J + 2 * R * N * O)
+
+F32 = mybir.dt.float32
+BF16 = mybir.dt.bfloat16
+I32 = mybir.dt.int32
+U32 = mybir.dt.uint32
+U16 = mybir.dt.uint16
+U8 = mybir.dt.uint8
+FP8X4 = mybir.dt.float8_e4m3fn_x4
+FP4X4 = mybir.dt.float4_e2m1fn_x4
+ACT = mybir.ActivationFunctionType
+ALU = mybir.AluOpType
+
+P = 128
+PACK = 4
+LANES = 16
+HALVES = 2
+JH = J // HALVES
+OH = O // HALVES
+NB = N // P
+
+
+def tile_picked_codes_plain_bank_mixedpair_outcomes_outboard_kernel(
+    tc, ta, ga, w_words, w_scales, xo_words, xo_scales, w2_words, w2_scales, sa, sb,
+    wb_words, wb_scales, wo_words, wo_scales, so, sp,
+    offs, offs2, offs3, offs4, offs5, offs6, offs7, out,
+):
+    nc = tc.nc
+    with ExitStack() as ctx:
+        keep = ctx.enter_context(tc.tile_pool(name="keep", bufs=1))
+        psum = ctx.enter_context(tc.psum_pool(name="psum", bufs=1))
+
+        def sbuf(name, shape, dtype):
+            return keep.tile(shape, dtype, name=name, align_bytes=64)
+
+        def load_list(name, src):
+            tile = keep.tile(list(src.shape), U16, name=name)
+            nc.sync.dma_start(tile[:], src)
+            return tile
+
+        def load_dealt_vector(name, src):
+            tile = sbuf(name, [P, PACK], F32)
+            nc.sync.dma_start(tile[:], src.rearrange("(p t) o -> p (t o)", t=PACK))
+            return tile
+
+        def load_block_vector(name, src):
+            tile = sbuf(name, [P, NB], F32)
+            with nc.allow_non_contiguous_dma(reason="one value a partition and block"):
+                nc.sync.dma_start(tile[:], src.rearrange("(b p) o -> p (b o)", p=P))
+            return tile
+
+        def load_words(name, src, width, dtype):
+            tile = sbuf(name, [P, width], dtype)
+            nc.sync.dma_start(tile[:].bitcast(I32), src.bitcast(I32))
+            return tile
+
+        def stage_scales(name, src):
+            rows = src.bitcast(I32).rearrange("(q i) n -> i q n", i=4)
+            stage = sbuf(name, [P, 2, rows.shape[2]], I32)
+            for pair in range(2):
+                nc.sync.dma_start(stage[64 * pair : 64 * pair + 4, :, :], rows[:, 2 * pair : 2 * pair + 2, :])
+            return stage
+
+        def zeroed_scales(name, width):
+            tile = sbuf(name, [P, width], U8)
+            nc.vector.memset(tile[:].bitcast(I32), 0)
+            return tile
+
+        def spread_scales(tile, stage):
+            for q in range(4):
+                first = 64 * (q // 2)
+                nc.vector.tensor_copy(tile[32 * q : 32 * q + 4, :].bitcast(I32), stage[first : first + 4, q % 2, :])
+
+        def load_scales_in_place(tile, src):
+            rows = src.bitcast(I32)
+            for q in range(4):
+                nc.sync.dma_start(tile[32 * q : 32 * q + 4, :].bitcast(I32), rows[4 * q : 4 * q + 4, :])
+
+        xo_sc = zeroed_scales("xo_sc", M)
+        w_sc_raw = zeroed_scales("w_sc_raw", R)
+        w2_sc_raw = zeroed_scales("w2_sc_raw", R)
+        wb_sc = zeroed_scales("wb_sc", N)
+        wo_sc = zeroed_scales("wo_sc", N)
+        board = [sbuf("board%d" % b, [P, E], F32) for b in range(NB)]
+        for b in range(NB):
+            nc.vector.memset(board[b][:], 0.0)
+
+        ta_rows = ta.rearrange("(p t) c -> p t c", t=PACK)
+        table = [sbuf("table%d" % t, [P, T], F32) for t in range(PACK)]
+
+        def load_table(t):
+            nc.sync.dma_start(table[t][:], ta_rows[:, t, :])
+
+        list1 = load_list("list1", offs)
+        ga_t = load_dealt_vector("ga_t", ga)
+        load_table(0)
+        list2 = load_list("list2", offs2)
+        xo_stage = stage_scales("xo_stage", xo_scales[0])
+        xo_w = load_words("xo_w", xo_words[0], M, U16)
+        load_table(1)
+        w_stage = stage_scales("w_stage", w_scales[0])
+        w2_stage = stage_scales("w2_stage", w2_scales[0])
+        w_raw = load_words("w_raw", w_words[0], R, U16)
+        load_table(2)
+        load_table(3)
+        w2_raw = load_words("w2_raw", w2_words[0].rearrange("p n t -> p (n t)"), R, U32)
+        list3 = load_list("list3", offs3)
+        list4 = load_list("list4", offs4)
+        sa_t = load_dealt_vector("sa_t", sa)
+        sb_t = load_dealt_vector("sb_t", sb)
+        wb_w = load_words("wb_w", wb_words[0].rearrange("p n t -> p (n t)"), N, U32)
+        wo_w = load_words("wo_w", wo_words[0], N, U16)
+        load_scales_in_place(wb_sc, wb_scales[0])
+        load_scales_in_place(wo_sc, wo_scales[0])
+        list5 = load_list("list5", offs5)
+        list7 = load_list("list7", offs7)
+        list6 = load_list("list6", offs6)
+        so_t = load_block_vector("so_t", so)
+        sp_t = load_block_vector("sp_t", sp)
+
+        xc_rows = [sbuf("xc_rows%d" % t, [P, J], BF16) for t in range(PACK)]
+        xc_in = [sbuf("xc_in%d" % h, [P, JH, PACK], BF16) for h in range(HALVES)]
+
+        def fetch_xc(t):
+            nc.scalar.activation(
+                out=xc_rows[t][:], in_=table[t][:].indirect(list1[:]), func=ACT.Copy, scale=ga_t[:, t : t + 1]
+            )
+            for h in range(HALVES):
+                nc.vector.tensor_copy(xc_in[h][:, :, t], xc_rows[t][:, h * JH : (h + 1) * JH])
+
+        fetch_xc(0)
+
+        spread_scales(xo_sc, xo_stage)
+        xo_gw = sbuf("xo_gw", [P, J], U16)
+        xo_gs = sbuf("xo_gs", [P, J], U8)
+        nc.vector.tensor_copy(xo_gw[:], xo_w[:].indirect(list2[:]))
+        nc.vector.tensor_copy(xo_gs[:], xo_sc[:].indirect(list2[:]))
+
+        fetch_xc(1)
+
+        spread_scales(w_sc_raw, w_stage)
+        spread_scales(w2_sc_raw, w2_stage)
+        w_sc = sbuf("w_sc", [P, PACK, P], U8)
+        w2_sc = sbuf("w2_sc", [P, PACK, P], U8)
+        w_w = sbuf("w_w", [P, PACK, P], U16)
+        w2_w = sbuf("w2_w", [P, PACK, P], U32)
+        nc.vector.tensor_copy(w_sc[:], w_sc_raw[:].rearrange("p (m t) -> p t m", t=PACK))
+        nc.vector.tensor_copy(w2_sc[:], w2_sc_raw[:].rearrange("p (m t) -> p t m", t=PACK))
+        nc.scalar.copy(w_w[:], w_raw[:].rearrange("p (m t) -> p t m", t=PACK))
+
+        fetch_xc(2)
+        nc.vector.tensor_copy(w2_w[:].rearrange("p t m -> p m t"), w2_raw[:].rearrange("p (m t) -> p m t", t=PACK))
+        fetch_xc(3)
+
+        xc_w = sbuf("xc_w", [P, J], U32)
+        xc_sc = sbuf("xc_sc", [P, J], U8)
+        for h in range(HALVES):
+            cols = slice(h * JH, (h + 1) * JH)
+            nc.vector.quantize_mx(
+                out=xc_w[:, cols].bitcast(FP8X4), scales=xc_sc[:, cols], in_=xc_in[h][:].rearrange("p j t -> p (j t)")
+            )
+
+        pieces = [(0, slice(h * JH, (h + 1) * JH)) for h in range(HALVES)] + [(t, slice(0, J)) for t in range(1, PACK)]
+        a_banks = [psum.tile([P, cols.stop - cols.start], F32, name="bank%d" % i) for i, (t, cols) in enumerate(pieces)]
+        a_rows = [sbuf("a_rows%d" % t, [P, J], F32) for t in range(PACK)]
+        for bank, (t, cols) in zip(a_banks, pieces):
+            nc.tensor.matmul_mx(
+                bank[:], lhsT=w2_w[:, t, :].bitcast(FP8X4), lhsT_scale=w2_sc[:, t, :],
+                rhs=xo_gw[:, cols].bitcast(FP4X4), rhs_scale=xo_gs[:, cols], start=True, stop=False,
+            )
+            nc.tensor.matmul_mx(
+                bank[:], lhsT=w_w[:, t, :].bitcast(FP4X4), lhsT_scale=w_sc[:, t, :],
+                rhs=xc_w[:, cols].bitcast(FP8X4), rhs_scale=xc_sc[:, cols], start=False, stop=True,
+            )
+            if t == 0:
+                nc.scalar.copy(a_rows[t][:, cols], bank[:])
+            else:
+                nc.vector.tensor_copy(a_rows[t][:, cols], bank[:])
+
+        slots = {(0, 0): 0, (0, 1): 1, (1, 0): 2, (2, 0): 3, (3, 0): 4, (1, 1): 3, (2, 1): 4, (3, 1): 2}
+        first = [sbuf("first%d" % i, [P, OH], F32) for i in range(5)]
+        second = [sbuf("second%d" % i, [P, OH], F32) for i in range(5)]
+        hid_rows = sbuf("hid_rows", [P, PACK + 1, OH], BF16)
+        hid_w = sbuf("hid_w", [P, O], U32)
+        hid_sc = sbuf("hid_sc", [P, O], U8)
+        p_rows = [sbuf("p_rows%d" % h, [P, NB, OH], F32) for h in range(HALVES)]
+        q_rows = [sbuf("q_rows%d" % b, [P, O], F32) for b in range(NB)]
+        p_banks = [psum.tile([P, NB, OH], F32, name="p_bank%d" % h) for h in range(HALVES)]
+        q_bank = psum.tile([P, NB, O], F32, name="q_bank")
+
+        def places(h):
+            return slice(h * OH // LANES, (h + 1) * OH // LANES)
+
+        def fetch_hid(t, h, diff):
+            nc.scalar.activation(
+                out=first[slots[(t, h)]][:], in_=a_rows[t][:].indirect(list3[:, places(h)]), func=ACT.Copy,
+                scale=sa_t[:, t : t + 1],
+            )
+            nc.scalar.activation(
+                out=second[slots[(t, h)]][:], in_=a_rows[t][:].indirect(list4[:, places(h)]), func=ACT.Copy,
+                scale=sb_t[:, t : t + 1],
+            )
+            nc.vector.tensor_tensor(diff, first[slots[(t, h)]][:], second[slots[(t, h)]][:], ALU.subtract)
+            nc.vector.scalar_tensor_tensor(hid_rows[:, 1 - h + t, :], diff, -1.0, diff, ALU.mult, ALU.max)
+
+        def first_outcome(h):
+            cols = slice(h * OH, (h + 1) * OH)
+            hid_in = sbuf("hid_in%d" % h, [P, OH, PACK], BF16)
+            nc.vector.tensor_copy(hid_in[:], hid_rows[:, 1 - h : 1 - h + PACK, :].rearrange("p t o -> p o t"))
+            nc.vector.quantize_mx(
+                out=hid_w[:, cols].bitcast(FP8X4), scales=hid_sc[:, cols], in_=hid_in[:].rearrange("p o t -> p (o t)")
+            )
+            for b in range(NB):
+                rows = slice(b * P, (b + 1) * P)
+                nc.tensor.matmul_mx(
+                    p_banks[h][:, b, :], lhsT=wb_w[:, rows].bitcast(FP8X4), lhsT_scale=wb_sc[:, rows],
+                    rhs=hid_w[:, cols].bitcast(FP8X4), rhs_scale=hid_sc[:, cols], start=True, stop=True,
+                )
+
+        diff_early = sbuf("diff_early", [P, 6, OH], F32)
+        fetch_hid(0, 0, diff_early[:, 0, :])
+        fetch_hid(0, 1, diff_early[:, 1, :])
+        for t in range(1, PACK):
+            fetch_hid(t, 0, diff_early[:, 1 + t, :])
+        first_outcome(0)
+        fetch_hid(1, 1, diff_early[:, 5, :])
+        diff_late = sbuf("hid_in0", [P, 2, OH], F32)
+        for t in range(2, PACK):
+            fetch_hid(t, 1, diff_late[:, t - 2, :])
+        first_outcome(1)
+        for b in range(NB):
+            rows = slice(b * P, (b + 1) * P)
+            nc.tensor.matmul_mx(
+                q_bank[:, b, :], lhsT=wo_w[:, rows].bitcast(FP4X4), lhsT_scale=wo_sc[:, rows],
+                rhs=hid_w[:].bitcast(FP8X4), rhs_scale=hid_sc[:], start=True, stop=True,
+            )
+
+        nc.scalar.copy(p_rows[0][:], p_banks[0][:])
+        for b in range(NB):
+            nc.scalar.activation(out=board[b][:].indirect(list5[:, places(0)]), in_=p_rows[0][:, b, :], func=ACT.Copy)
+        nc.vector.tensor_copy(p_rows[1][:], p_banks[1][:])
+        for b in range(NB):
+            nc.vector.tensor_copy(board[b][:].indirect(list5[:, places(1)]), p_rows[1][:, b, :])
+        for b in range(NB):
+            nc.scalar.copy(q_rows[b][:], q_bank[:, b, :])
+
+        from_q = [sbuf("from_q%d" % b, [P, U], F32) for b in range(NB)]
+        from_board = [sbuf("from_board%d" % b, [P, U], F32) for b in range(NB)]
+        larger = [sbuf("larger%d" % b, [P, U], F32) for b in range(NB)]
+        for b in range(NB):
+            nc.scalar.activation(
+                out=from_q[b][:], in_=q_rows[b][:].indirect(list7[:]), func=ACT.Copy, scale=sp_t[:, b : b + 1]
+            )
+        for b in range(NB):
+            nc.scalar.activation(
+                out=from_board[b][:], in_=board[b][:].indirect(list6[:]), func=ACT.Copy, scale=so_t[:, b : b + 1]
+            )
+            nc.vector.tensor_tensor(larger[b][:], from_board[b][:], from_q[b][:], ALU.max)
+            nc.sync.dma_start(out[b * P : (b + 1) * P, :], larger[b][:])

@@ -96,42 +96,46 @@ def tile_picked_codes_plain_bank_mixedpair_outcomes_outboard_kernel(
         def load_table(t):
             nc.sync.dma_start(table[t][:], ta_rows[:, t, :])
 
+        load_table(0)
         list1 = load_list("list1", offs)
         ga_t = load_dealt_vector("ga_t", ga)
-        load_table(0)
         list2 = load_list("list2", offs2)
         xo_stage = stage_scales("xo_stage", xo_scales[0])
         xo_w = load_words("xo_w", xo_words[0], M, U16)
         load_table(1)
         w_stage = stage_scales("w_stage", w_scales[0])
         w2_stage = stage_scales("w2_stage", w2_scales[0])
-        w_raw = load_words("w_raw", w_words[0], R, U16)
         load_table(2)
         load_table(3)
         w2_raw = load_words("w2_raw", w2_words[0].rearrange("p n t -> p (n t)"), R, U32)
+        w_raw = load_words("w_raw", w_words[0], R, U16)
         list3 = load_list("list3", offs3)
         list4 = load_list("list4", offs4)
         sa_t = load_dealt_vector("sa_t", sa)
         sb_t = load_dealt_vector("sb_t", sb)
-        wb_w = load_words("wb_w", wb_words[0].rearrange("p n t -> p (n t)"), N, U32)
-        wo_w = load_words("wo_w", wo_words[0], N, U16)
-        load_scales_in_place(wb_sc, wb_scales[0])
-        load_scales_in_place(wo_sc, wo_scales[0])
         list5 = load_list("list5", offs5)
+        wb_w = load_words("wb_w", wb_words[0].rearrange("p n t -> p (n t)"), N, U32)
+        load_scales_in_place(wb_sc, wb_scales[0])
+        wo_w = load_words("wo_w", wo_words[0], N, U16)
+        load_scales_in_place(wo_sc, wo_scales[0])
         list7 = load_list("list7", offs7)
+        sp_t = load_block_vector("sp_t", sp)
         list6 = load_list("list6", offs6)
         so_t = load_block_vector("so_t", so)
-        sp_t = load_block_vector("sp_t", sp)
 
-        xc_rows = [sbuf("xc_rows%d" % t, [P, J], BF16) for t in range(PACK)]
+        xc_rows = sbuf("xc_rows", [P, PACK, J], BF16)
         xc_in = [sbuf("xc_in%d" % h, [P, JH, PACK], BF16) for h in range(HALVES)]
 
         def fetch_xc(t):
             nc.scalar.activation(
-                out=xc_rows[t][:], in_=table[t][:].indirect(list1[:]), func=ACT.Copy, scale=ga_t[:, t : t + 1]
+                out=xc_rows[:, t, :], in_=table[t][:].indirect(list1[:]), func=ACT.Copy, scale=ga_t[:, t : t + 1]
             )
+
+        def weave_xc(rows):
             for h in range(HALVES):
-                nc.vector.tensor_copy(xc_in[h][:, :, t], xc_rows[t][:, h * JH : (h + 1) * JH])
+                nc.vector.tensor_copy(
+                    xc_in[h][:, :, rows], xc_rows[:, rows, h * JH : (h + 1) * JH].rearrange("p t j -> p j t")
+                )
 
         fetch_xc(0)
 
@@ -151,103 +155,110 @@ def tile_picked_codes_plain_bank_mixedpair_outcomes_outboard_kernel(
         w2_w = sbuf("w2_w", [P, PACK, P], U32)
         nc.vector.tensor_copy(w_sc[:], w_sc_raw[:].rearrange("p (m t) -> p t m", t=PACK))
         nc.vector.tensor_copy(w2_sc[:], w2_sc_raw[:].rearrange("p (m t) -> p t m", t=PACK))
-        nc.scalar.copy(w_w[:], w_raw[:].rearrange("p (m t) -> p t m", t=PACK))
 
         fetch_xc(2)
+        weave_xc(slice(0, PACK - 1))
         nc.vector.tensor_copy(w2_w[:].rearrange("p t m -> p m t"), w2_raw[:].rearrange("p (m t) -> p m t", t=PACK))
         fetch_xc(3)
+        weave_xc(slice(PACK - 1, PACK))
+        nc.scalar.copy(w_w[:], w_raw[:].rearrange("p (m t) -> p t m", t=PACK))
 
         xc_w = sbuf("xc_w", [P, J], U32)
         xc_sc = sbuf("xc_sc", [P, J], U8)
-        for h in range(HALVES):
-            cols = slice(h * JH, (h + 1) * JH)
+        stretches = [slice(0, JH), slice(JH, JH + JH // 2), slice(JH + JH // 2, J)]
+        for cols in stretches:
+            h = cols.start // JH
+            woven = xc_in[h][:, cols.start - h * JH : cols.stop - h * JH, :]
             nc.vector.quantize_mx(
-                out=xc_w[:, cols].bitcast(FP8X4), scales=xc_sc[:, cols], in_=xc_in[h][:].rearrange("p j t -> p (j t)")
+                out=xc_w[:, cols].bitcast(FP8X4), scales=xc_sc[:, cols], in_=woven.rearrange("p j t -> p (j t)")
             )
 
-        pieces = [(0, slice(h * JH, (h + 1) * JH)) for h in range(HALVES)] + [(t, slice(0, J)) for t in range(1, PACK)]
+        pieces = [(0, cols) for cols in stretches] + [(t, slice(0, J)) for t in range(1, PACK)]
         a_banks = [psum.tile([P, cols.stop - cols.start], F32, name="bank%d" % i) for i, (t, cols) in enumerate(pieces)]
         a_rows = [sbuf("a_rows%d" % t, [P, J], F32) for t in range(PACK)]
         for bank, (t, cols) in zip(a_banks, pieces):
-            nc.tensor.matmul_mx(
-                bank[:], lhsT=w2_w[:, t, :].bitcast(FP8X4), lhsT_scale=w2_sc[:, t, :],
-                rhs=xo_gw[:, cols].bitcast(FP4X4), rhs_scale=xo_gs[:, cols], start=True, stop=False,
-            )
-            nc.tensor.matmul_mx(
-                bank[:], lhsT=w_w[:, t, :].bitcast(FP4X4), lhsT_scale=w_sc[:, t, :],
-                rhs=xc_w[:, cols].bitcast(FP8X4), rhs_scale=xc_sc[:, cols], start=False, stop=True,
-            )
+            notes_pass = (w2_w[:, t, :].bitcast(FP8X4), w2_sc[:, t, :], xo_gw[:, cols].bitcast(FP4X4), xo_gs[:, cols])
+            codes_pass = (w_w[:, t, :].bitcast(FP4X4), w_sc[:, t, :], xc_w[:, cols].bitcast(FP8X4), xc_sc[:, cols])
+            passes = (notes_pass, codes_pass) if t < 2 else (codes_pass, notes_pass)
+            for i, (lhs, lhs_sc, rhs, rhs_sc) in enumerate(passes):
+                nc.tensor.matmul_mx(
+                    bank[:], lhsT=lhs, lhsT_scale=lhs_sc, rhs=rhs, rhs_scale=rhs_sc, start=(i == 0), stop=(i == 1)
+                )
             if t == 0:
                 nc.scalar.copy(a_rows[t][:, cols], bank[:])
             else:
                 nc.vector.tensor_copy(a_rows[t][:, cols], bank[:])
 
-        slots = {(0, 0): 0, (0, 1): 1, (1, 0): 2, (2, 0): 3, (3, 0): 4, (1, 1): 3, (2, 1): 4, (3, 1): 2}
-        first = [sbuf("first%d" % i, [P, OH], F32) for i in range(5)]
-        second = [sbuf("second%d" % i, [P, OH], F32) for i in range(5)]
-        hid_rows = sbuf("hid_rows", [P, PACK + 1, OH], BF16)
+        first = sbuf("first", [P, PACK, OH], F32)
+        second = sbuf("second", [P, PACK, OH], F32)
+        diff = sbuf("diff", [P, 2, 2, OH], F32)
         hid_w = sbuf("hid_w", [P, O], U32)
         hid_sc = sbuf("hid_sc", [P, O], U8)
-        p_rows = [sbuf("p_rows%d" % h, [P, NB, OH], F32) for h in range(HALVES)]
         q_rows = [sbuf("q_rows%d" % b, [P, O], F32) for b in range(NB)]
-        p_banks = [psum.tile([P, NB, OH], F32, name="p_bank%d" % h) for h in range(HALVES)]
-        q_bank = psum.tile([P, NB, O], F32, name="q_bank")
 
         def places(h):
             return slice(h * OH // LANES, (h + 1) * OH // LANES)
 
-        def fetch_hid(t, h, diff):
-            nc.scalar.activation(
-                out=first[slots[(t, h)]][:], in_=a_rows[t][:].indirect(list3[:, places(h)]), func=ACT.Copy,
-                scale=sa_t[:, t : t + 1],
-            )
-            nc.scalar.activation(
-                out=second[slots[(t, h)]][:], in_=a_rows[t][:].indirect(list4[:, places(h)]), func=ACT.Copy,
-                scale=sb_t[:, t : t + 1],
-            )
-            nc.vector.tensor_tensor(diff, first[slots[(t, h)]][:], second[slots[(t, h)]][:], ALU.subtract)
-            nc.vector.scalar_tensor_tensor(hid_rows[:, 1 - h + t, :], diff, -1.0, diff, ALU.mult, ALU.max)
-
-        def first_outcome(h):
-            cols = slice(h * OH, (h + 1) * OH)
+        def hid_half(h):
             hid_in = sbuf("hid_in%d" % h, [P, OH, PACK], BF16)
-            nc.vector.tensor_copy(hid_in[:], hid_rows[:, 1 - h : 1 - h + PACK, :].rearrange("p t o -> p o t"))
+            for pair in range(2):
+                pair_diff = first[:, 0:2, :] if (h, pair) == (1, 1) else diff[:, pair + h, :, :]
+                for i in range(2):
+                    t = 2 * pair + i
+                    nc.scalar.activation(
+                        out=first[:, t, :], in_=a_rows[t][:].indirect(list3[:, places(h)]), func=ACT.Copy,
+                        scale=sa_t[:, t : t + 1],
+                    )
+                    nc.scalar.activation(
+                        out=second[:, t, :], in_=a_rows[t][:].indirect(list4[:, places(h)]), func=ACT.Copy,
+                        scale=sb_t[:, t : t + 1],
+                    )
+                    nc.vector.tensor_tensor(pair_diff[:, i, :], first[:, t, :], second[:, t, :], ALU.subtract)
+                woven = pair_diff.rearrange("p i o -> p o i")
+                nc.vector.scalar_tensor_tensor(
+                    hid_in[:, :, 2 * pair : 2 * pair + 2], woven, -1.0, woven, ALU.mult, ALU.max
+                )
+            cols = slice(h * OH, (h + 1) * OH)
             nc.vector.quantize_mx(
                 out=hid_w[:, cols].bitcast(FP8X4), scales=hid_sc[:, cols], in_=hid_in[:].rearrange("p o t -> p (o t)")
             )
-            for b in range(NB):
-                rows = slice(b * P, (b + 1) * P)
-                nc.tensor.matmul_mx(
-                    p_banks[h][:, b, :], lhsT=wb_w[:, rows].bitcast(FP8X4), lhsT_scale=wb_sc[:, rows],
-                    rhs=hid_w[:, cols].bitcast(FP8X4), rhs_scale=hid_sc[:, cols], start=True, stop=True,
-                )
 
-        diff_early = sbuf("diff_early", [P, 6, OH], F32)
-        fetch_hid(0, 0, diff_early[:, 0, :])
-        fetch_hid(0, 1, diff_early[:, 1, :])
-        for t in range(1, PACK):
-            fetch_hid(t, 0, diff_early[:, 1 + t, :])
-        first_outcome(0)
-        fetch_hid(1, 1, diff_early[:, 5, :])
-        diff_late = sbuf("hid_in0", [P, 2, OH], F32)
-        for t in range(2, PACK):
-            fetch_hid(t, 1, diff_late[:, t - 2, :])
-        first_outcome(1)
-        for b in range(NB):
+        def outcome(h, b, words, scales, packed, bank):
+            cols = slice(h * OH, (h + 1) * OH)
             rows = slice(b * P, (b + 1) * P)
             nc.tensor.matmul_mx(
-                q_bank[:, b, :], lhsT=wo_w[:, rows].bitcast(FP4X4), lhsT_scale=wo_sc[:, rows],
-                rhs=hid_w[:].bitcast(FP8X4), rhs_scale=hid_sc[:], start=True, stop=True,
+                bank, lhsT=words[:, rows].bitcast(packed), lhsT_scale=scales[:, rows],
+                rhs=hid_w[:, cols].bitcast(FP8X4), rhs_scale=hid_sc[:, cols], start=True, stop=True,
             )
 
-        nc.scalar.copy(p_rows[0][:], p_banks[0][:])
+        hid_half(0)
+        p_bank0 = psum.tile([P, NB, OH], F32, name="p_bank0")
+        q_bank0 = psum.tile([P, NB, OH], F32, name="q_bank0")
         for b in range(NB):
-            nc.scalar.activation(out=board[b][:].indirect(list5[:, places(0)]), in_=p_rows[0][:, b, :], func=ACT.Copy)
-        nc.vector.tensor_copy(p_rows[1][:], p_banks[1][:])
+            outcome(0, b, wb_w, wb_sc, FP8X4, p_bank0[:, b, :])
         for b in range(NB):
-            nc.vector.tensor_copy(board[b][:].indirect(list5[:, places(1)]), p_rows[1][:, b, :])
+            outcome(0, b, wo_w, wo_sc, FP4X4, q_bank0[:, b, :])
+        hid_half(1)
+        p_banks1 = [psum.tile([P, OH], F32, name="bank%d" % b) for b in range(NB)]
+        q_bank1 = psum.tile([P, NB, OH], F32, name="bank%d" % NB)
         for b in range(NB):
-            nc.scalar.copy(q_rows[b][:], q_bank[:, b, :])
+            outcome(1, b, wb_w, wb_sc, FP8X4, p_banks1[b][:])
+        for b in range(NB):
+            outcome(1, b, wo_w, wo_sc, FP4X4, q_bank1[:, b, :])
+
+        p0 = sbuf("p0", [P, NB, OH], F32)
+        nc.scalar.copy(p0[:], p_bank0[:])
+        for b in range(NB):
+            nc.scalar.activation(out=board[b][:].indirect(list5[:, places(0)]), in_=p0[:, b, :], func=ACT.Copy)
+        for b in range(NB):
+            nc.scalar.copy(q_rows[b][:, 0:OH], q_bank0[:, b, :])
+        p1 = [sbuf("p1%d" % b, [P, OH], F32) for b in range(NB)]
+        nc.vector.tensor_copy(p1[0][:], p_banks1[0][:])
+        nc.scalar.copy(p1[1][:], p_banks1[1][:])
+        for b in range(NB):
+            nc.vector.tensor_copy(board[b][:].indirect(list5[:, places(1)]), p1[b][:])
+        for b in range(NB):
+            nc.scalar.copy(q_rows[b][:, OH:O], q_bank1[:, b, :])
 
         from_q = [sbuf("from_q%d" % b, [P, U], F32) for b in range(NB)]
         from_board = [sbuf("from_board%d" % b, [P, U], F32) for b in range(NB)]

from contextlib import ExitStack

import concourse.mybir as mybir

K, J, R, T, Z, M, O, N, U, E = 512, 512, 512, 2048, 512, 1024, 256, 256, 128, 512
FLOPS = 2 * (K * R * J + Z * R * J + 2 * R * N * O)

F32 = mybir.dt.float32
BF16 = mybir.dt.bfloat16
I32 = mybir.dt.int32
U32 = mybir.dt.uint32
U16 = mybir.dt.uint16
U8 = mybir.dt.uint8
FP8X4 = mybir.dt.float8_e4m3fn_x4
FP4X4 = mybir.dt.float4_e2m1fn_x4
ACT = mybir.ActivationFunctionType
ALU = mybir.AluOpType

P = 128
PACK = 4
LANES = 16
HALVES = 2
JH = J // HALVES
OH = O // HALVES
NB = N // P


def tile_picked_codes_plain_bank_mixedpair_outcomes_outboard_kernel(
    tc, ta, ga, w_words, w_scales, xo_words, xo_scales, w2_words, w2_scales, sa, sb,
    wb_words, wb_scales, wo_words, wo_scales, so, sp,
    offs, offs2, offs3, offs4, offs5, offs6, offs7, out,
):
    nc = tc.nc
    with ExitStack() as ctx:
        keep = ctx.enter_context(tc.tile_pool(name="keep", bufs=1))
        psum = ctx.enter_context(tc.psum_pool(name="psum", bufs=1))

        def sbuf(name, shape, dtype):
            return keep.tile(shape, dtype, name=name, align_bytes=64)

        def load_list(name, src):
            tile = keep.tile(list(src.shape), U16, name=name)
            nc.sync.dma_start(tile[:], src)
            return tile

        def load_dealt_vector(name, src):
            tile = sbuf(name, [P, PACK], F32)
            nc.sync.dma_start(tile[:], src.rearrange("(p t) o -> p (t o)", t=PACK))
            return tile

        def load_block_vector(name, src):
            tile = sbuf(name, [P, NB], F32)
            with nc.allow_non_contiguous_dma(reason="one value a partition and block"):
                nc.sync.dma_start(tile[:], src.rearrange("(b p) o -> p (b o)", p=P))
            return tile

        def load_words(name, src, width, dtype):
            tile = sbuf(name, [P, width], dtype)
            nc.sync.dma_start(tile[:].bitcast(I32), src.bitcast(I32))
            return tile

        def stage_scales(name, src):
            rows = src.bitcast(I32).rearrange("(q i) n -> i q n", i=4)
            stage = sbuf(name, [P, 2, rows.shape[2]], I32)
            for pair in range(2):
                nc.sync.dma_start(stage[64 * pair : 64 * pair + 4, :, :], rows[:, 2 * pair : 2 * pair + 2, :])
            return stage

        def zeroed_scales(name, width):
            tile = sbuf(name, [P, width], U8)
            nc.vector.memset(tile[:].bitcast(I32), 0)
            return tile

        def spread_scales(tile, stage):
            for q in range(4):
                first = 64 * (q // 2)
                nc.vector.tensor_copy(tile[32 * q : 32 * q + 4, :].bitcast(I32), stage[first : first + 4, q % 2, :])

        def load_scales_in_place(tile, src):
            rows = src.bitcast(I32)
            for q in range(4):
                nc.sync.dma_start(tile[32 * q : 32 * q + 4, :].bitcast(I32), rows[4 * q : 4 * q + 4, :])

        xo_sc = zeroed_scales("xo_sc", M)
        w_sc_raw = zeroed_scales("w_sc_raw", R)
        w2_sc_raw = zeroed_scales("w2_sc_raw", R)
        wb_sc = zeroed_scales("wb_sc", N)
        wo_sc = zeroed_scales("wo_sc", N)
        board = [sbuf("board%d" % b, [P, E], F32) for b in range(NB)]
        for b in range(NB):
            nc.vector.memset(board[b][:], 0.0)

        ta_rows = ta.rearrange("(p t) c -> p t c", t=PACK)
        table = [sbuf("table%d" % t, [P, T], F32) for t in range(PACK)]

        def load_table(t):
            nc.sync.dma_start(table[t][:], ta_rows[:, t, :])

        load_table(0)
        list1 = load_list("list1", offs)
        ga_t = load_dealt_vector("ga_t", ga)
        list2 = load_list("list2", offs2)
        xo_stage = stage_scales("xo_stage", xo_scales[0])
        xo_w = load_words("xo_w", xo_words[0], M, U16)
        load_table(1)
        w_stage = stage_scales("w_stage", w_scales[0])
        w2_stage = stage_scales("w2_stage", w2_scales[0])
        load_table(2)
        load_table(3)
        w2_raw = load_words("w2_raw", w2_words[0].rearrange("p n t -> p (n t)"), R, U32)
        w_raw = load_words("w_raw", w_words[0], R, U16)
        list3 = load_list("list3", offs3)
        list4 = load_list("list4", offs4)
        sa_t = load_dealt_vector("sa_t", sa)
        sb_t = load_dealt_vector("sb_t", sb)
        list5 = load_list("list5", offs5)
        wb_w = load_words("wb_w", wb_words[0].rearrange("p n t -> p (n t)"), N, U32)
        load_scales_in_place(wb_sc, wb_scales[0])
        wo_w = load_words("wo_w", wo_words[0], N, U16)
        load_scales_in_place(wo_sc, wo_scales[0])
        list7 = load_list("list7", offs7)
        sp_t = load_block_vector("sp_t", sp)
        list6 = load_list("list6", offs6)
        so_t = load_block_vector("so_t", so)

        xc_rows = sbuf("xc_rows", [P, PACK, J], BF16)
        xc_in = [sbuf("xc_in%d" % h, [P, JH, PACK], BF16) for h in range(HALVES)]

        def fetch_xc(t):
            nc.scalar.activation(
                out=xc_rows[:, t, :], in_=table[t][:].indirect(list1[:]), func=ACT.Copy, scale=ga_t[:, t : t + 1]
            )

        def weave_xc(rows):
            for h in range(HALVES):
                nc.vector.tensor_copy(
                    xc_in[h][:, :, rows], xc_rows[:, rows, h * JH : (h + 1) * JH].rearrange("p t j -> p j t")
                )

        fetch_xc(0)

        spread_scales(xo_sc, xo_stage)
        xo_gw = sbuf("xo_gw", [P, J], U16)
        xo_gs = sbuf("xo_gs", [P, J], U8)
        nc.vector.tensor_copy(xo_gw[:], xo_w[:].indirect(list2[:]))
        nc.vector.tensor_copy(xo_gs[:], xo_sc[:].indirect(list2[:]))

        fetch_xc(1)

        spread_scales(w_sc_raw, w_stage)
        spread_scales(w2_sc_raw, w2_stage)
        w_sc = sbuf("w_sc", [P, PACK, P], U8)
        w2_sc = sbuf("w2_sc", [P, PACK, P], U8)
        w_w = sbuf("w_w", [P, PACK, P], U16)
        w2_w = sbuf("w2_w", [P, PACK, P], U32)
        nc.vector.tensor_copy(w_sc[:], w_sc_raw[:].rearrange("p (m t) -> p t m", t=PACK))
        nc.vector.tensor_copy(w2_sc[:], w2_sc_raw[:].rearrange("p (m t) -> p t m", t=PACK))

        fetch_xc(2)
        weave_xc(slice(0, PACK - 1))
        nc.vector.tensor_copy(w2_w[:].rearrange("p t m -> p m t"), w2_raw[:].rearrange("p (m t) -> p m t", t=PACK))
        fetch_xc(3)
        weave_xc(slice(PACK - 1, PACK))
        nc.scalar.copy(w_w[:], w_raw[:].rearrange("p (m t) -> p t m", t=PACK))

        xc_w = sbuf("xc_w", [P, J], U32)
        xc_sc = sbuf("xc_sc", [P, J], U8)
        stretches = [slice(0, JH), slice(JH, JH + JH // 2), slice(JH + JH // 2, J)]
        for cols in stretches:
            h = cols.start // JH
            woven = xc_in[h][:, cols.start - h * JH : cols.stop - h * JH, :]
            nc.vector.quantize_mx(
                out=xc_w[:, cols].bitcast(FP8X4), scales=xc_sc[:, cols], in_=woven.rearrange("p j t -> p (j t)")
            )

        pieces = [(0, cols) for cols in stretches] + [(t, slice(0, J)) for t in range(1, PACK)]
        a_banks = [psum.tile([P, cols.stop - cols.start], F32, name="bank%d" % i) for i, (t, cols) in enumerate(pieces)]
        a_rows = [sbuf("a_rows%d" % t, [P, J], F32) for t in range(PACK)]
        for bank, (t, cols) in zip(a_banks, pieces):
            notes_pass = (w2_w[:, t, :].bitcast(FP8X4), w2_sc[:, t, :], xo_gw[:, cols].bitcast(FP4X4), xo_gs[:, cols])
            codes_pass = (w_w[:, t, :].bitcast(FP4X4), w_sc[:, t, :], xc_w[:, cols].bitcast(FP8X4), xc_sc[:, cols])
            passes = (notes_pass, codes_pass) if t < 2 else (codes_pass, notes_pass)
            for i, (lhs, lhs_sc, rhs, rhs_sc) in enumerate(passes):
                nc.tensor.matmul_mx(
                    bank[:], lhsT=lhs, lhsT_scale=lhs_sc, rhs=rhs, rhs_scale=rhs_sc, start=(i == 0), stop=(i == 1)
                )
            if t == 0:
                nc.scalar.copy(a_rows[t][:, cols], bank[:])
            else:
                nc.vector.tensor_copy(a_rows[t][:, cols], bank[:])

        first = sbuf("first", [P, PACK, OH], F32)
        second = sbuf("second", [P, PACK, OH], F32)
        diff = sbuf("diff", [P, 2, 2, OH], F32)
        hid_w = sbuf("hid_w", [P, O], U32)
        hid_sc = sbuf("hid_sc", [P, O], U8)
        q_rows = [sbuf("q_rows%d" % b, [P, O], F32) for b in range(NB)]

        def places(h):
            return slice(h * OH // LANES, (h + 1) * OH // LANES)

        def hid_half(h):
            hid_in = sbuf("hid_in%d" % h, [P, OH, PACK], BF16)
            for pair in range(2):
                pair_diff = first[:, 0:2, :] if (h, pair) == (1, 1) else diff[:, pair + h, :, :]
                for i in range(2):
                    t = 2 * pair + i
                    nc.scalar.activation(
                        out=first[:, t, :], in_=a_rows[t][:].indirect(list3[:, places(h)]), func=ACT.Copy,
                        scale=sa_t[:, t : t + 1],
                    )
                    nc.scalar.activation(
                        out=second[:, t, :], in_=a_rows[t][:].indirect(list4[:, places(h)]), func=ACT.Copy,
                        scale=sb_t[:, t : t + 1],
                    )
                    nc.vector.tensor_tensor(pair_diff[:, i, :], first[:, t, :], second[:, t, :], ALU.subtract)
                woven = pair_diff.rearrange("p i o -> p o i")
                nc.vector.scalar_tensor_tensor(
                    hid_in[:, :, 2 * pair : 2 * pair + 2], woven, -1.0, woven, ALU.mult, ALU.max
                )
            cols = slice(h * OH, (h + 1) * OH)
            nc.vector.quantize_mx(
                out=hid_w[:, cols].bitcast(FP8X4), scales=hid_sc[:, cols], in_=hid_in[:].rearrange("p o t -> p (o t)")
            )

        def outcome(h, b, words, scales, packed, bank):
            cols = slice(h * OH, (h + 1) * OH)
            rows = slice(b * P, (b + 1) * P)
            nc.tensor.matmul_mx(
                bank, lhsT=words[:, rows].bitcast(packed), lhsT_scale=scales[:, rows],
                rhs=hid_w[:, cols].bitcast(FP8X4), rhs_scale=hid_sc[:, cols], start=True, stop=True,
            )

        hid_half(0)
        p_bank0 = psum.tile([P, NB, OH], F32, name="p_bank0")
        q_bank0 = psum.tile([P, NB, OH], F32, name="q_bank0")
        for b in range(NB):
            outcome(0, b, wb_w, wb_sc, FP8X4, p_bank0[:, b, :])
        for b in range(NB):
            outcome(0, b, wo_w, wo_sc, FP4X4, q_bank0[:, b, :])
        hid_half(1)
        p_banks1 = [psum.tile([P, OH], F32, name="bank%d" % b) for b in range(NB)]
        q_bank1 = psum.tile([P, NB, OH], F32, name="bank%d" % NB)
        for b in range(NB):
            outcome(1, b, wb_w, wb_sc, FP8X4, p_banks1[b][:])
        for b in range(NB):
            outcome(1, b, wo_w, wo_sc, FP4X4, q_bank1[:, b, :])

        p0 = sbuf("p0", [P, NB, OH], F32)
        nc.scalar.copy(p0[:], p_bank0[:])
        for b in range(NB):
            nc.scalar.activation(out=board[b][:].indirect(list5[:, places(0)]), in_=p0[:, b, :], func=ACT.Copy)
        for b in range(NB):
            nc.scalar.copy(q_rows[b][:, 0:OH], q_bank0[:, b, :])
        p1 = [sbuf("p1%d" % b, [P, OH], F32) for b in range(NB)]
        nc.vector.tensor_copy(p1[0][:], p_banks1[0][:])
        nc.scalar.copy(p1[1][:], p_banks1[1][:])
        for b in range(NB):
            nc.vector.tensor_copy(board[b][:].indirect(list5[:, places(1)]), p1[b][:])
        for b in range(NB):
            nc.scalar.copy(q_rows[b][:, OH:O], q_bank1[:, b, :])

        from_q = [sbuf("from_q%d" % b, [P, U], F32) for b in range(NB)]
        from_board = [sbuf("from_board%d" % b, [P, U], F32) for b in range(NB)]
        larger = [sbuf("larger%d" % b, [P, U], F32) for b in range(NB)]
        for b in range(NB):
            nc.scalar.activation(
                out=from_q[b][:], in_=q_rows[b][:].indirect(list7[:]), func=ACT.Copy, scale=sp_t[:, b : b + 1]
            )
        for b in range(NB):
            nc.scalar.activation(
                out=from_board[b][:], in_=board[b][:].indirect(list6[:]), func=ACT.Copy, scale=so_t[:, b : b + 1]
            )
            nc.vector.tensor_tensor(larger[b][:], from_board[b][:], from_q[b][:], ALU.max)
            nc.sync.dma_start(out[b * P : (b + 1) * P, :], larger[b][:])
